import numpy as np
import ml_dtypes


def mxq(x, axis, fmt="e4m3"):
    dtype, down = {"e4m3": (ml_dtypes.float8_e4m3fn, 7), "e5m2": (ml_dtypes.float8_e5m2, 14)}[fmt]
    v = np.moveaxis(np.asarray(x, np.float32).astype(ml_dtypes.bfloat16).astype(np.float64), axis, -1)
    blocks = v.reshape(v.shape[:-1] + (-1, 32))
    amax = np.abs(blocks).max(-1, keepdims=True)
    byte = np.maximum(np.where(amax > 0, np.frexp(amax)[1] - 1 + 127, 0) - down, 1)
    scale = np.exp2(byte - 127.0)
    codes = (blocks / scale).astype(np.float32).astype(dtype).astype(np.float64)
    return np.moveaxis((codes * scale).reshape(v.shape), -1, axis)


WIDE = False


def mx_kscale(k):
    if not WIDE:
        return np.ones(k)
    levels = np.array([10, -10, 5, -5, 0])
    if k % 512:
        return np.exp2(np.random.permutation(np.resize(levels, k // 32))).repeat(32)
    a = np.empty((k // 512, 16))
    for p in range(k // 512):
        a[p, :8] = np.random.permutation(np.resize(levels, 8))
        for g in range(8):
            far = levels[np.abs(levels - a[p, g]) >= 10]
            a[p, g + 8] = far[np.random.randint(len(far))]
    return np.exp2(a.ravel()).repeat(32)


def f64(x):
    return np.asarray(x).astype(np.float64)


def striped(idx):
    return np.tile(idx.reshape(-1, 16).T, (8, 1)).astype(np.uint16)


def unstriped(offs):
    return offs[:16].T.reshape(-1).astype(np.int64)


E2M1 = np.array([0.0, 0.5, 1.0, 1.5, 2.0, 3.0, 4.0, 6.0, -0.0, -0.5, -1.0, -1.5, -2.0, -3.0, -4.0, -6.0])


def pack_weight(w, fmt):
    k, n = w.shape
    w = f64(np.asarray(w, np.float32).astype(ml_dtypes.bfloat16)).reshape(k // 32, 32, n)
    amax = np.abs(w).max(1)
    if fmt == "e4m3":
        byte = np.frexp(amax)[1] - 1 + 127 - 7
    else:
        mant, ex = np.frexp(amax / 6.0)
        byte = np.where(mant > 0.5, ex, ex - 1) + 127
    byte = np.clip(np.where(amax > 0, byte, 1), 1, 254)
    scaled = (w * np.exp2(127.0 - byte)[:, None, :]).reshape(k, n).astype(np.float32)
    by_word = np.ascontiguousarray(scaled.reshape(k // 512, 128, 4, n).transpose(0, 1, 3, 2))
    if fmt == "e4m3":
        words = by_word.astype(ml_dtypes.float8_e4m3fn).view(np.uint8)
    else:
        c = by_word.astype(ml_dtypes.float4_e2m1fn).view(np.uint8) & 0xF
        words = (c[..., 0::2] | (c[..., 1::2] << 4)).reshape(k // 512, 128, 2 * n)
    return np.ascontiguousarray(words), np.ascontiguousarray(byte.astype(np.uint8).reshape(k // 512, 16, n))


def unpack_weight(words, scales, fmt):
    g, _, n = scales.shape
    words = np.ascontiguousarray(words).reshape(g, 128, n, -1)
    if fmt == "e4m3":
        vals = words.view(ml_dtypes.float8_e4m3fn).astype(np.float64)
    else:
        nib = np.empty((g, 128, n, 4), np.uint8)
        nib[..., 0::2] = words & 0xF
        nib[..., 1::2] = words >> 4
        vals = E2M1[nib]
    vals = vals * np.repeat(np.exp2(scales.astype(np.float64) - 127.0), 8, axis=1)[..., None]
    return vals.transpose(0, 1, 3, 2).reshape(g * 512, n)


def gelu(v):
    return 0.5 * v * (1.0 + np.tanh(np.sqrt(2.0 / np.pi) * (v + 0.044715 * v**3)))


K, H, N, T, S = 1024, 512, 256, 4096, 1024

def setup_inputs():
    n = np.random.standard_normal
    s = mx_kscale(K)[:, None]
    u = mx_kscale(H)[:, None]
    tab_words, tab_scales = pack_weight(n((K, T)) * s, "e2m1")
    w1 = 1.2 * n((K, H)) / np.sqrt(K) / s
    w2_words, w2_scales = pack_weight(1.3 * n((K, H)) / np.sqrt(K) / s, "e4m3")
    w3 = 2.0 * n((K, H)) / np.sqrt(K) / s * u.T
    w4_words, w4_scales = pack_weight(1.5 * n((H, N)) / np.sqrt(H) / u, "e2m1")
    return {
        "tab_words": tab_words, "tab_scales": tab_scales,
        "offs": striped(np.random.permutation(T)[:S]),
        "offs2": striped(np.random.permutation(T)[:S]),
        "w1": w1.astype(np.float32),
        "w2_words": w2_words, "w2_scales": w2_scales,
        "w3": w3.astype(np.float32),
        "w4_words": w4_words, "w4_scales": w4_scales,
        "bo": (0.4 * n(N)).astype(np.float32),
    }

def reference(tab_words, tab_scales, offs, offs2, w1, w2_words, w2_scales, w3, w4_words, w4_scales, bo):
    TW = unpack_weight(tab_words, tab_scales, "e2m1")
    v = TW[:, unstriped(offs)]
    v2 = TW[:, unstriped(offs2)]
    w2 = unpack_weight(w2_words, w2_scales, "e4m3")
    w4 = unpack_weight(w4_words, w4_scales, "e2m1")
    a = np.tanh(mxq(f64(w1), 0, "e4m3").T @ v)
    b = w2.T @ v2
    d = b / (1.0 + np.exp(-b)) * (mxq(f64(w3), 0, "e4m3").T @ v2)
    h = mxq(a * d, 0, "e4m3")
    return (w4.T @ h) + f64(bo)[:, None]

@@ -1,0 +1,256 @@
+from contextlib import ExitStack
+
+import concourse.mybir as mybir
+
+K, H, N, T, S = 1024, 512, 256, 4096, 1024
+FLOPS = 2 * S * (3 * K * H + H * N)
+
+F32 = mybir.dt.float32
+BF16 = mybir.dt.bfloat16
+I32 = mybir.dt.int32
+U16 = mybir.dt.uint16
+U8 = mybir.dt.uint8
+FP8X4 = mybir.dt.float8_e4m3fn_x4
+FP4X4 = mybir.dt.float4_e2m1fn_x4
+ACT = mybir.ActivationFunctionType
+MULT = mybir.AluOpType.mult
+ADD = mybir.AluOpType.add
+
+P = 128
+PACK = 4
+PASSES = K // (P * PACK)
+HALF = 512
+HALVES = S // HALF
+TILE = 128
+TILES = HALF // TILE
+LIVE = 100
+SHIFT = 16
+
+
+def tile_list_retraction_exposure_scores_kernel(
+    tc, tab_words, tab_scales, offs, offs2, w1, w2_words, w2_scales, w3, w4_words, w4_scales, bo, out
+):
+    nc = tc.nc
+    with ExitStack() as ctx:
+        keep = ctx.enter_context(tc.tile_pool(name="keep", bufs=1))
+        ring = ctx.enter_context(tc.tile_pool(name="ring", bufs=8))
+        psum = ctx.enter_context(tc.psum_pool(name="psum", bufs=1))
+        reused = ctx.enter_context(tc.tile_pool(name="reused", bufs=1))
+
+        def held(name, shape, dtype, place=None):
+            if place is None:
+                return keep.tile(shape, dtype, name=name, align_bytes=64)
+            return reused.tile(shape, dtype, name=name, align_bytes=64, offset=place)
+
+        places = {"w2": 0, (1, 0): 4096, (1, 1): 8192, (3, 0): 12288, (3, 1): 16384}
+
+        citing = keep.tile([P, S // 16], U16, name="citing")
+        retracted = keep.tile([P, S // 16], U16, name="retracted")
+        table = [held("table%d" % a, [P, T], U16) for a in range(PASSES)]
+        table_scales = held("table_scales", [P, T], U8)
+        second = held("second", [P, 2 * S], U8)
+        w2_raw = held("w2_raw", [P, PASSES * H], I32, places["w2"])
+        w2_raw_scales = held("w2_raw_scales", [P, PASSES * H], U8)
+        w2_codes = held("w2_codes", [P, PASSES * H], I32)
+        w2_planes = held("w2_planes", [P, PASSES * H], U8)
+        w4_codes = held("w4_codes", [P, 2 * N], U8)
+        w4_plane = held("w4_plane", [P, N], U8)
+        bias = held("bias", [P, N // P], F32)
+        raw = {}
+
+        idle = held("idle", [P, 2], F32)
+        nc.gpsimd.memset(idle[:, 0:1], 0.0)
+        nc.scalar.activation(out=idle[:, 1:2], in_=idle[:, 0:1], func=ACT.Silu)
+        nc.vector.memset(table_scales[:].bitcast(I32), 0)
+        nc.vector.memset(w2_raw_scales[:].bitcast(I32), 0)
+        nc.vector.memset(second[:].bitcast(I32), 0)
+        nc.vector.memset(w4_plane[:].bitcast(I32), 0)
+
+        def load_table(a):
+            nc.sync.dma_start(out=table[a][:].bitcast(I32), in_=tab_words[a].bitcast(I32))
+
+        def load_weight(w, a):
+            raw[w, a] = keep.tile([P, PACK, H], F32, name="raw%d" % a, align_bytes=64)
+            rows = (w1 if w == 1 else w3)[a * P * PACK : (a + 1) * P * PACK, :]
+            nc.sync.dma_start(out=raw[w, a][:], in_=rows.rearrange("(p j) c -> p j c", j=PACK))
+
+        def load_w2():
+            nc.sync.dma_start(
+                out=w2_raw[:].rearrange("p (a c) -> p a c", a=PASSES),
+                in_=w2_words.rearrange("a p c i -> p a (c i)").bitcast(I32),
+            )
+
+        nc.sync.dma_start(citing[:], offs)
+        load_table(0)
+        nc.sync.dma_start(retracted[:], offs2)
+        rows = tab_scales.bitcast(I32).rearrange("a (q r) c -> r q a c", r=4)
+        for r in range(4):
+            nc.gpsimd.dma_start(out=table_scales[r:P:SHIFT, :].bitcast(I32), in_=rows[r])
+        rows = w2_scales.bitcast(I32).rearrange("a r c -> r a c")
+        for q in range(4):
+            nc.scalar.dma_start(
+                out=w2_raw_scales[32 * q : 32 * q + 4, :].bitcast(I32).rearrange("p (a c) -> p a c", a=PASSES),
+                in_=rows[4 * q : 4 * q + 4],
+            )
+        load_weight(1, 0)
+        load_weight(1, 1)
+        load_table(1)
+        load_w2()
+        lists = (citing, retracted)
+        words, planes, grouped, codes, scales = {}, {}, {}, {}, {}
+
+        def piece(which, half):
+            return lists[which][:, half * HALF // 16 : (half + 1) * HALF // 16]
+
+        def gather_words(which, a, half, place=None):
+            picked = held("words%d%d%d" % (which, a, half), [P, HALF], U16, place)
+            nc.vector.tensor_copy(picked[:], table[a][:].indirect(piece(which, half)))
+            words[which, a, half] = picked
+
+        def gather_scales(which, half, place=None):
+            picked = held("picked_scales%d%d" % (which, half), [P, HALF], U8, place)
+            nc.vector.tensor_copy(picked[:], table_scales[:].indirect(piece(which, half)))
+            start = (which * HALVES + half) * HALF
+            nc.gpsimd.dma_start(
+                out=second[0:LIVE, start : start + HALF].bitcast(I32),
+                in_=picked[SHIFT : SHIFT + LIVE, :].bitcast(I32),
+            )
+            planes[which, 0, half] = picked[:]
+            planes[which, 1, half] = second[:, start : start + HALF]
+
+        def cast(w, a, engine):
+            rounded = held("rounded%d%d" % (w, a), [P, PACK * H], BF16, places[w, a])
+            src = raw[w, a][:].rearrange("p j (m t) -> p m j t", t=PACK)
+            dst = rounded[:].rearrange("p (t m j) -> p m j t", t=PACK, j=PACK)
+            if engine == "scalar":
+                nc.scalar.copy(out=dst, in_=src)
+            elif engine == "vector":
+                nc.vector.tensor_copy(out=dst, in_=src)
+            else:
+                nc.gpsimd.tensor_scalar(dst, src, 1.0, 0.0, MULT, ADD)
+            grouped[w, a] = rounded
+
+        def quantize(w, a):
+            c = held("codes%d%d" % (w, a), [P, H], I32)
+            s = held("scales%d%d" % (w, a), [P, H], U8)
+            nc.vector.quantize_mx(out=c[:].bitcast(FP8X4), scales=s[:], in_=grouped[w, a][:])
+            codes[w, a], scales[w, a] = c[:], s[:]
+
+        def order_w2():
+            for dst, src in ((w2_planes, w2_raw_scales), (w2_codes, w2_raw)):
+                nc.vector.tensor_copy(
+                    out=dst[:].rearrange("p (a t m) -> p a m t", a=PASSES, t=PACK),
+                    in_=src[:].rearrange("p (a m t) -> p a m t", a=PASSES, t=PACK),
+                )
+            for a in range(PASSES):
+                codes[2, a] = w2_codes[:, a * H : (a + 1) * H]
+                scales[2, a] = w2_planes[:, a * H : (a + 1) * H]
+
+        def product(w, which, half, i):
+            bank = psum.tile([P, PACK, TILE], F32, name="bank", tag="bank", bufs=6)
+            cols = slice(i * TILE, (i + 1) * TILE)
+            for t in range(PACK):
+                m = slice(t * P, (t + 1) * P)
+                for a in range(PASSES):
+                    nc.tensor.matmul_mx(
+                        out=bank[:, t, :],
+                        lhsT=codes[w, a][:, m].bitcast(FP8X4),
+                        lhsT_scale=scales[w, a][:, m],
+                        rhs=words[which, a, half][:, cols].bitcast(FP4X4),
+                        rhs_scale=planes[which, a, half][:, cols],
+                        start=(a == 0),
+                        stop=(a == PASSES - 1),
+                    )
+            return bank[:].rearrange("p t n -> p n t")
+
+        def woven(tile):
+            return tile.rearrange("p (n t) -> p n t", t=PACK)
+
+        gate, stance = {}, {}
+
+        def activate(store, w, which, func, half):
+            for i in range(TILES):
+                sums = product(w, which, half, i)
+                value = held("value%d%d%d" % (w, half, i), [P, PACK * TILE], F32)
+                nc.scalar.activation(out=woven(value[:]), in_=sums, func=func)
+                store[half, i] = value
+
+        h = [held("h%d" % q, [P, PACK * 2 * TILE], BF16) for q in range(4)]
+
+        def combine(half, i, engine):
+            both = ring.tile([P, PACK * TILE], F32, name="both")
+            engine.tensor_tensor(both[:], gate[half, i][:], stance[half, i][:], MULT)
+            sums = product(3, 1, half, i)
+            part = h[2 * half + i // 2][:, (i % 2) * PACK * TILE : (i % 2 + 1) * PACK * TILE]
+            nc.vector.tensor_tensor(woven(part), sums, woven(both[:]), MULT)
+
+        def finish(q):
+            width = 2 * TILE
+            h_codes = held("h_codes%d" % q, [P, width], I32)
+            h_plane = held("h_plane%d" % q, [P, width], U8)
+            nc.vector.quantize_mx(out=h_codes[:].bitcast(FP8X4), scales=h_plane[:], in_=h[q][:])
+            result = [held("result%d%d" % (q, c), [P, width], F32) for c in range(N // P)]
+            for c in range(N // P):
+                last = psum.tile([P, width], F32, name="last", tag="last", bufs=2)
+                nc.tensor.matmul_mx(
+                    out=last[:],
+                    lhsT=w4_codes[:, 2 * P * c : 2 * P * (c + 1)].bitcast(FP4X4),
+                    lhsT_scale=w4_plane[:, P * c : P * (c + 1)],
+                    rhs=h_codes[:].bitcast(FP8X4),
+                    rhs_scale=h_plane[:],
+                    start=True,
+                    stop=True,
+                )
+                if c == 0 or q < 3:
+                    nc.scalar.activation(out=result[c][:], in_=last[:], func=ACT.Identity, bias=bias[:, c : c + 1])
+                else:
+                    nc.vector.tensor_scalar(result[c][:], last[:], bias[:, c : c + 1], None, ADD)
+                nc.sync.dma_start(out=out[c * P : (c + 1) * P, q * width : (q + 1) * width], in_=result[c][:])
+
+        gather_words(0, 0, 0)
+        gather_words(1, 0, 0)
+        cast(1, 0, "scalar")
+        cast(1, 1, "scalar")
+        load_weight(3, 0)
+        load_weight(3, 1)
+        nc.sync.dma_start(out=w4_codes[:].bitcast(I32), in_=w4_words[0].bitcast(I32))
+        for q in range(4):
+            nc.sync.dma_start(
+                out=w4_plane[32 * q : 32 * q + 4, :].bitcast(I32), in_=w4_scales[0].bitcast(I32)[4 * q : 4 * q + 4, :]
+            )
+        with nc.allow_non_contiguous_dma(reason="one bias value a partition"):
+            nc.sync.dma_start(out=bias[:], in_=bo.rearrange("(c p) -> p c", p=P))
+
+        gather_scales(0, 0)
+        gather_scales(1, 0)
+        quantize(1, 0)
+        gather_words(0, 0, 1, places[1, 0])
+        gather_words(0, 1, 0)
+        quantize(1, 1)
+        activate(stance, 1, 0, ACT.Tanh, 0)
+        gather_words(1, 1, 0, places[1, 1])
+        order_w2()
+        cast(3, 0, "scalar")
+        activate(gate, 2, 1, ACT.Silu, 0)
+        gather_scales(0, 1, places["w2"])
+        gather_words(0, 1, 1, places["w2"] + 1024)
+        gather_scales(1, 1, places["w2"] + 512)
+        gather_words(1, 0, 1, places["w2"] + 2048)
+        gather_words(1, 1, 1, places["w2"] + 3072)
+        activate(stance, 1, 0, ACT.Tanh, 1)
+        activate(gate, 2, 1, ACT.Silu, 1)
+        cast(3, 1, "vector")
+        quantize(3, 0)
+        quantize(3, 1)
+        combine(0, 0, nc.gpsimd)
+        combine(0, 1, nc.gpsimd)
+        combine(0, 2, nc.gpsimd)
+        finish(0)
+        combine(0, 3, nc.gpsimd)
+        combine(1, 0, nc.gpsimd)
+        finish(1)
+        combine(1, 1, nc.gpsimd)
+        combine(1, 2, nc.gpsimd)
+        finish(2)
+        combine(1, 3, nc.gpsimd)
+        finish(3)

@@ -20,11 +20,19 @@ P = 128
 PACK = 4
 PASSES = K // (P * PACK)
 HALF = 512
-HALVES = S // HALF
 TILE = 128
 TILES = HALF // TILE
 LIVE = 100
 SHIFT = 16
+
+TABLE_B = 0
+W2_SCALES = 8192
+RAW_B = 9216
+RAW_A = RAW_B + 8192
+RAW_LAST = RAW_A + 8192
+SCALE_TABLE = RAW_LAST + 8192 - 64
+W2_RAW = SCALE_TABLE + 3712
+ROUNDED = W2_RAW + 4096
 
 
 def tile_list_retraction_exposure_scores_kernel(
@@ -33,122 +41,73 @@ def tile_list_retraction_exposure_scores_kernel(
     nc = tc.nc
     with ExitStack() as ctx:
         keep = ctx.enter_context(tc.tile_pool(name="keep", bufs=1))
-        ring = ctx.enter_context(tc.tile_pool(name="ring", bufs=8))
-        psum = ctx.enter_context(tc.psum_pool(name="psum", bufs=1))
         reused = ctx.enter_context(tc.tile_pool(name="reused", bufs=1))
+        psum = ctx.enter_context(tc.psum_pool(name="psum", bufs=1))
 
         def held(name, shape, dtype, place=None):
             if place is None:
                 return keep.tile(shape, dtype, name=name, align_bytes=64)
             return reused.tile(shape, dtype, name=name, align_bytes=64, offset=place)
 
-        places = {"w2": 0, (1, 0): 4096, (1, 1): 8192, (3, 0): 12288, (3, 1): 16384}
-
         citing = keep.tile([P, S // 16], U16, name="citing")
         retracted = keep.tile([P, S // 16], U16, name="retracted")
-        table = [held("table%d" % a, [P, T], U16) for a in range(PASSES)]
-        table_scales = held("table_scales", [P, T], U8)
-        second = held("second", [P, 2 * S], U8)
-        w2_raw = held("w2_raw", [P, PASSES * H], I32, places["w2"])
-        w2_raw_scales = held("w2_raw_scales", [P, PASSES * H], U8)
+        lists = (citing, retracted)
+        idle_in = held("idle_in", [P, 32], F32, RAW_A - 64)
+        idle_out = held("idle_out", [P, 32], F32, W2_SCALES - 64)
+        nc.gpsimd.memset(idle_in[:], 0.0)
+        nc.scalar.activation(out=idle_out[:], in_=idle_in[:], func=ACT.Silu)
+        table = [held("table0", [P, T], U16), held("table1", [P, T], U16, TABLE_B)]
+        table_scales = held("table_scales", [P, T], U8, SCALE_TABLE)
+        picked_scales = held("picked_scales", [P, 2 * S], U8)
+        moved_scales = held("moved_scales", [P, 2 * S], U8)
+        w2_raw_scales = held("w2_raw_scales", [P, PASSES * H], U8, W2_SCALES)
         w2_codes = held("w2_codes", [P, PASSES * H], I32)
         w2_planes = held("w2_planes", [P, PASSES * H], U8)
-        w4_codes = held("w4_codes", [P, 2 * N], U8)
-        w4_plane = held("w4_plane", [P, N], U8)
-        bias = held("bias", [P, N // P], F32)
-        raw = {}
+        planes = (picked_scales, moved_scales)
+        raw, words, rounded, codes, scales, gate, stance = {}, {}, {}, {}, {}, {}, {}
+        rounded_place = {(w, a): ROUNDED + 4096 * (w - 1 + a) for w in (1, 3) for a in range(PASSES)}
 
-        idle = held("idle", [P, 2], F32)
-        nc.gpsimd.memset(idle[:, 0:1], 0.0)
-        nc.scalar.activation(out=idle[:, 1:2], in_=idle[:, 0:1], func=ACT.Silu)
         nc.vector.memset(table_scales[:].bitcast(I32), 0)
+        nc.vector.memset(moved_scales[:].bitcast(I32), 0)
         nc.vector.memset(w2_raw_scales[:].bitcast(I32), 0)
-        nc.vector.memset(second[:].bitcast(I32), 0)
-        nc.vector.memset(w4_plane[:].bitcast(I32), 0)
 
         def load_table(a):
             nc.sync.dma_start(out=table[a][:].bitcast(I32), in_=tab_words[a].bitcast(I32))
 
-        def load_weight(w, a):
-            raw[w, a] = keep.tile([P, PACK, H], F32, name="raw%d" % a, align_bytes=64)
+        def load_weight(w, a, place):
+            raw[w, a] = held("raw%d%d" % (w, a), [P, PACK, H], F32, place)
             rows = (w1 if w == 1 else w3)[a * P * PACK : (a + 1) * P * PACK, :]
             nc.sync.dma_start(out=raw[w, a][:], in_=rows.rearrange("(p j) c -> p j c", j=PACK))
 
-        def load_w2():
-            nc.sync.dma_start(
-                out=w2_raw[:].rearrange("p (a c) -> p a c", a=PASSES),
-                in_=w2_words.rearrange("a p c i -> p a (c i)").bitcast(I32),
-            )
-
-        nc.sync.dma_start(citing[:], offs)
-        load_table(0)
-        nc.sync.dma_start(retracted[:], offs2)
-        rows = tab_scales.bitcast(I32).rearrange("a (q r) c -> r q a c", r=4)
-        for r in range(4):
-            nc.gpsimd.dma_start(out=table_scales[r:P:SHIFT, :].bitcast(I32), in_=rows[r])
-        rows = w2_scales.bitcast(I32).rearrange("a r c -> r a c")
-        for q in range(4):
-            nc.scalar.dma_start(
-                out=w2_raw_scales[32 * q : 32 * q + 4, :].bitcast(I32).rearrange("p (a c) -> p a c", a=PASSES),
-                in_=rows[4 * q : 4 * q + 4],
-            )
-        load_weight(1, 0)
-        load_weight(1, 1)
-        load_table(1)
-        load_w2()
-        lists = (citing, retracted)
-        words, planes, grouped, codes, scales = {}, {}, {}, {}, {}
-
-        def piece(which, half):
-            return lists[which][:, half * HALF // 16 : (half + 1) * HALF // 16]
-
         def gather_words(which, a, half, place=None):
             picked = held("words%d%d%d" % (which, a, half), [P, HALF], U16, place)
-            nc.vector.tensor_copy(picked[:], table[a][:].indirect(piece(which, half)))
+            piece = lists[which][:, half * HALF // 16 : (half + 1) * HALF // 16]
+            nc.vector.tensor_copy(picked[:], table[a][:].indirect(piece))
             words[which, a, half] = picked
 
-        def gather_scales(which, half, place=None):
-            picked = held("picked_scales%d%d" % (which, half), [P, HALF], U8, place)
-            nc.vector.tensor_copy(picked[:], table_scales[:].indirect(piece(which, half)))
-            start = (which * HALVES + half) * HALF
-            nc.gpsimd.dma_start(
-                out=second[0:LIVE, start : start + HALF].bitcast(I32),
-                in_=picked[SHIFT : SHIFT + LIVE, :].bitcast(I32),
+        def cast(w, a):
+            rounded[w, a] = held("rounded%d%d" % (w, a), [P, PACK * H], BF16, rounded_place[w, a])
+            nc.scalar.copy(
+                out=rounded[w, a][:].rearrange("p (t m j) -> p m j t", t=PACK, j=PACK),
+                in_=raw[w, a][:].rearrange("p j (m t) -> p m j t", t=PACK),
             )
-            planes[which, 0, half] = picked[:]
-            planes[which, 1, half] = second[:, start : start + HALF]
 
-        def cast(w, a, engine):
-            rounded = held("rounded%d%d" % (w, a), [P, PACK * H], BF16, places[w, a])
-            src = raw[w, a][:].rearrange("p j (m t) -> p m j t", t=PACK)
-            dst = rounded[:].rearrange("p (t m j) -> p m j t", t=PACK, j=PACK)
-            if engine == "scalar":
-                nc.scalar.copy(out=dst, in_=src)
-            elif engine == "vector":
-                nc.vector.tensor_copy(out=dst, in_=src)
-            else:
-                nc.gpsimd.tensor_scalar(dst, src, 1.0, 0.0, MULT, ADD)
-            grouped[w, a] = rounded
-
-        def quantize(w, a):
-            c = held("codes%d%d" % (w, a), [P, H], I32)
-            s = held("scales%d%d" % (w, a), [P, H], U8)
-            nc.vector.quantize_mx(out=c[:].bitcast(FP8X4), scales=s[:], in_=grouped[w, a][:])
+        def quantize(w, a, place=None):
+            c = held("codes%d%d" % (w, a), [P, H], I32, place)
+            s = held("scales%d%d" % (w, a), [P, H], U8, None if place is None else place + 2048)
+            nc.vector.quantize_mx(out=c[:].bitcast(FP8X4), scales=s[:], in_=rounded[w, a][:])
             codes[w, a], scales[w, a] = c[:], s[:]
 
-        def order_w2():
-            for dst, src in ((w2_planes, w2_raw_scales), (w2_codes, w2_raw)):
-                nc.vector.tensor_copy(
-                    out=dst[:].rearrange("p (a t m) -> p a m t", a=PASSES, t=PACK),
-                    in_=src[:].rearrange("p (a m t) -> p a m t", a=PASSES, t=PACK),
-                )
-            for a in range(PASSES):
-                codes[2, a] = w2_codes[:, a * H : (a + 1) * H]
-                scales[2, a] = w2_planes[:, a * H : (a + 1) * H]
+        def reorder(dst, src):
+            nc.vector.tensor_copy(
+                out=dst[:].rearrange("p (a t m) -> p a m t", a=PASSES, t=PACK),
+                in_=src[:].rearrange("p (a m t) -> p a m t", a=PASSES, t=PACK),
+            )
 
         def product(w, which, half, i):
-            bank = psum.tile([P, PACK, TILE], F32, name="bank", tag="bank", bufs=6)
+            bank = psum.tile([P, PACK, TILE], F32, name="bank", tag="bank", bufs=7)
             cols = slice(i * TILE, (i + 1) * TILE)
+            start = which * S + half * HALF + i * TILE
             for t in range(PACK):
                 m = slice(t * P, (t + 1) * P)
                 for a in range(PASSES):
@@ -157,7 +116,7 @@ def tile_list_retraction_exposure_scores_kernel(
                         lhsT=codes[w, a][:, m].bitcast(FP8X4),
                         lhsT_scale=scales[w, a][:, m],
                         rhs=words[which, a, half][:, cols].bitcast(FP4X4),
-                        rhs_scale=planes[which, a, half][:, cols],
+                        rhs_scale=planes[a][:, start : start + TILE],
                         start=(a == 0),
                         stop=(a == PASSES - 1),
                     )
@@ -166,34 +125,32 @@ def tile_list_retraction_exposure_scores_kernel(
         def woven(tile):
             return tile.rearrange("p (n t) -> p n t", t=PACK)
 
-        gate, stance = {}, {}
+        def values(name, place=None):
+            return held(name, [P, PACK * HALF], F32, place)
 
-        def activate(store, w, which, func, half):
-            for i in range(TILES):
-                sums = product(w, which, half, i)
-                value = held("value%d%d%d" % (w, half, i), [P, PACK * TILE], F32)
-                nc.scalar.activation(out=woven(value[:]), in_=sums, func=func)
-                store[half, i] = value
+        def part(tile, i):
+            return tile[:, i * PACK * TILE : (i + 1) * PACK * TILE]
+
+        def activate(into, w, which, func, half, i):
+            nc.scalar.activation(out=woven(part(into, i)), in_=product(w, which, half, i), func=func)
 
         h = [held("h%d" % q, [P, PACK * 2 * TILE], BF16) for q in range(4)]
 
-        def combine(half, i, engine):
-            both = ring.tile([P, PACK * TILE], F32, name="both")
-            engine.tensor_tensor(both[:], gate[half, i][:], stance[half, i][:], MULT)
+        def combine(half, i, engine, place=None):
+            both = held("both%d%d" % (half, i), [P, PACK * TILE], F32, place)
+            engine.tensor_tensor(both[:], part(gate[half], i), part(stance[half], i), MULT)
             sums = product(3, 1, half, i)
-            part = h[2 * half + i // 2][:, (i % 2) * PACK * TILE : (i % 2 + 1) * PACK * TILE]
-            nc.vector.tensor_tensor(woven(part), sums, woven(both[:]), MULT)
+            nc.vector.tensor_tensor(woven(part(h[2 * half + i // 2], i % 2)), sums, woven(both[:]), MULT)
 
         def finish(q):
             width = 2 * TILE
             h_codes = held("h_codes%d" % q, [P, width], I32)
             h_plane = held("h_plane%d" % q, [P, width], U8)
             nc.vector.quantize_mx(out=h_codes[:].bitcast(FP8X4), scales=h_plane[:], in_=h[q][:])
-            result = [held("result%d%d" % (q, c), [P, width], F32) for c in range(N // P)]
+            last = psum.tile([P, N // P, width], F32, name="last", tag="last", bufs=1)
             for c in range(N // P):
-                last = psum.tile([P, width], F32, name="last", tag="last", bufs=2)
                 nc.tensor.matmul_mx(
-                    out=last[:],
+                    out=last[:, c, :],
                     lhsT=w4_codes[:, 2 * P * c : 2 * P * (c + 1)].bitcast(FP4X4),
                     lhsT_scale=w4_plane[:, P * c : P * (c + 1)],
                     rhs=h_codes[:].bitcast(FP8X4),
@@ -201,18 +158,57 @@ def tile_list_retraction_exposure_scores_kernel(
                     start=True,
                     stop=True,
                 )
-                if c == 0 or q < 3:
-                    nc.scalar.activation(out=result[c][:], in_=last[:], func=ACT.Identity, bias=bias[:, c : c + 1])
-                else:
-                    nc.vector.tensor_scalar(result[c][:], last[:], bias[:, c : c + 1], None, ADD)
-                nc.sync.dma_start(out=out[c * P : (c + 1) * P, q * width : (q + 1) * width], in_=result[c][:])
+            result = held("result%d" % q, [P, N // P, width], F32)
+            for c in range(N // P):
+                nc.scalar.activation(out=result[:, c, :], in_=last[:, c, :], func=ACT.Identity, bias=bias[:, c : c + 1])
+            nc.sync.dma_start(
+                out=out.rearrange("(c p) j -> p c j", p=P)[:, :, q * width : (q + 1) * width], in_=result[:]
+            )
+
+        nc.sync.dma_start(citing[:], offs)
+        load_table(0)
+        nc.sync.dma_start(retracted[:], offs2)
+        rows = tab_scales.bitcast(I32).rearrange("a (q r) c -> r q a c", r=4)
+        for r in range(4):
+            nc.sync.dma_start(out=table_scales[r:P:SHIFT, :].bitcast(I32), in_=rows[r])
+        load_weight(1, 0, RAW_A)
+        load_weight(1, 1, RAW_B)
+        load_table(1)
+        rows = w2_scales.bitcast(I32).rearrange("a r c -> r a c")
+        for q in range(4):
+            nc.sync.dma_start(
+                out=w2_raw_scales[32 * q : 32 * q + 4, :].bitcast(I32).rearrange("p (a c) -> p a c", a=PASSES),
+                in_=rows[4 * q : 4 * q + 4],
+            )
 
         gather_words(0, 0, 0)
         gather_words(1, 0, 0)
-        cast(1, 0, "scalar")
-        cast(1, 1, "scalar")
-        load_weight(3, 0)
-        load_weight(3, 1)
+        cast(1, 0)
+        load_weight(3, 0, RAW_A)
+        cast(1, 1)
+        for which in range(2):
+            nc.vector.tensor_copy(picked_scales[:, which * S : (which + 1) * S], table_scales[:].indirect(lists[which][:]))
+        nc.sync.dma_start(
+            out=moved_scales[0:LIVE, :].bitcast(I32), in_=picked_scales[SHIFT : SHIFT + LIVE, :].bitcast(I32)
+        )
+        w2_raw = held("w2_raw", [P, PASSES * H], I32, W2_RAW)
+        nc.sync.dma_start(
+            out=w2_raw[:].rearrange("p (a c) -> p a c", a=PASSES),
+            in_=w2_words.rearrange("a p c i -> p a (c i)").bitcast(I32),
+        )
+        load_weight(3, 1, RAW_LAST)
+        quantize(1, 0, SCALE_TABLE + 128)
+        gather_words(0, 1, 0, SCALE_TABLE + 2688)
+        quantize(1, 1)
+        stance[0] = values("stance0")
+        for i in range(TILES):
+            activate(stance[0], 1, 0, ACT.Tanh, 0, i)
+        gather_words(1, 1, 0, rounded_place[1, 1])
+
+        w4_codes = held("w4_codes", [P, 2 * N], U8, rounded_place[1, 1] + 1024)
+        w4_plane = held("w4_plane", [P, N], U8, rounded_place[1, 1] + 1536)
+        bias = held("bias", [P, N // P], F32, rounded_place[1, 1] + 1792)
+        nc.vector.memset(w4_plane[:].bitcast(I32), 0)
         nc.sync.dma_start(out=w4_codes[:].bitcast(I32), in_=w4_words[0].bitcast(I32))
         for q in range(4):
             nc.sync.dma_start(
@@ -221,36 +217,38 @@ def tile_list_retraction_exposure_scores_kernel(
         with nc.allow_non_contiguous_dma(reason="one bias value a partition"):
             nc.sync.dma_start(out=bias[:], in_=bo.rearrange("(c p) -> p c", p=P))
 
-        gather_scales(0, 0)
-        gather_scales(1, 0)
-        quantize(1, 0)
-        gather_words(0, 0, 1, places[1, 0])
-        gather_words(0, 1, 0)
-        quantize(1, 1)
-        activate(stance, 1, 0, ACT.Tanh, 0)
-        gather_words(1, 1, 0, places[1, 1])
-        order_w2()
-        cast(3, 0, "scalar")
-        activate(gate, 2, 1, ACT.Silu, 0)
-        gather_scales(0, 1, places["w2"])
-        gather_words(0, 1, 1, places["w2"] + 1024)
-        gather_scales(1, 1, places["w2"] + 512)
-        gather_words(1, 0, 1, places["w2"] + 2048)
-        gather_words(1, 1, 1, places["w2"] + 3072)
-        activate(stance, 1, 0, ACT.Tanh, 1)
-        activate(gate, 2, 1, ACT.Silu, 1)
-        cast(3, 1, "vector")
+        reorder(w2_planes, w2_raw_scales)
+        reorder(w2_codes, w2_raw)
+        for a in range(PASSES):
+            codes[2, a] = w2_codes[:, a * H : (a + 1) * H]
+            scales[2, a] = w2_planes[:, a * H : (a + 1) * H]
+        cast(3, 0)
+        cast(3, 1)
+        gate[0] = values("gate0", RAW_LAST + 64)
+        for i in range(TILES):
+            activate(gate[0], 2, 1, ACT.Silu, 0, i)
+        for which in range(2):
+            for a in range(PASSES):
+                gather_words(which, a, 1, W2_RAW + 1024 * (2 * which + a))
         quantize(3, 0)
         quantize(3, 1)
-        combine(0, 0, nc.gpsimd)
-        combine(0, 1, nc.gpsimd)
-        combine(0, 2, nc.gpsimd)
+        stance[1] = values("stance1", RAW_A + 64)
+        gate[1] = values("gate1")
+        for i in range(TILES):
+            activate(stance[1], 1, 0, ACT.Tanh, 1, i)
+        activate(gate[1], 2, 1, ACT.Silu, 1, 0)
+        activate(gate[1], 2, 1, ACT.Silu, 1, 1)
+        combine(0, 0, nc.vector, rounded_place[3, 1] + 0)
+        activate(gate[1], 2, 1, ACT.Silu, 1, 2)
+        combine(0, 1, nc.vector, rounded_place[3, 1] + 2048)
+        activate(gate[1], 2, 1, ACT.Silu, 1, 3)
+        combine(0, 2, nc.vector, rounded_place[3, 0] + 0)
         finish(0)
-        combine(0, 3, nc.gpsimd)
-        combine(1, 0, nc.gpsimd)
+        combine(0, 3, nc.vector, rounded_place[3, 0] + 2048)
+        combine(1, 0, nc.vector)
         finish(1)
-        combine(1, 1, nc.gpsimd)
-        combine(1, 2, nc.gpsimd)
+        combine(1, 1, nc.vector)
+        combine(1, 2, nc.vector)
         finish(2)
-        combine(1, 3, nc.gpsimd)
+        combine(1, 3, nc.vector)
         finish(3)

@@ -88,8 +88,8 @@ def tile_list_retraction_exposure_scores_kernel(
         def cast(w, a):
             rounded[w, a] = held("rounded%d%d" % (w, a), [P, PACK * H], BF16, rounded_place[w, a])
             nc.scalar.copy(
-                out=rounded[w, a][:].rearrange("p (t m j) -> p m j t", t=PACK, j=PACK),
-                in_=raw[w, a][:].rearrange("p j (m t) -> p m j t", t=PACK),
+                out=rounded[w, a][:].rearrange("p (u v m j) -> p u m j v", u=2, v=2, j=PACK),
+                in_=raw[w, a][:].rearrange("p j (m u v) -> p u m j v", u=2, v=2),
             )
 
         def quantize(w, a, place=None):
@@ -97,12 +97,6 @@ def tile_list_retraction_exposure_scores_kernel(
             s = held("scales%d%d" % (w, a), [P, H], U8, None if place is None else place + 2048)
             nc.vector.quantize_mx(out=c[:].bitcast(FP8X4), scales=s[:], in_=rounded[w, a][:])
             codes[w, a], scales[w, a] = c[:], s[:]
-
-        def reorder(dst, src):
-            nc.vector.tensor_copy(
-                out=dst[:].rearrange("p (a t m) -> p a m t", a=PASSES, t=PACK),
-                in_=src[:].rearrange("p (a m t) -> p a m t", a=PASSES, t=PACK),
-            )
 
         def product(w, which, half, i):
             bank = psum.tile([P, PACK, TILE], F32, name="bank", tag="bank", bufs=7)
@@ -136,37 +130,62 @@ def tile_list_retraction_exposure_scores_kernel(
 
         h = [held("h%d" % q, [P, PACK * 2 * TILE], BF16) for q in range(4)]
 
-        def combine(half, i, engine, place=None):
-            both = held("both%d%d" % (half, i), [P, PACK * TILE], F32, place)
-            engine.tensor_tensor(both[:], part(gate[half], i), part(stance[half], i), MULT)
-            sums = product(3, 1, half, i)
-            nc.vector.tensor_tensor(woven(part(h[2 * half + i // 2], i % 2)), sums, woven(both[:]), MULT)
+        both = {}
+
+        def pair(n, engine, place=None):
+            half, i = divmod(n, TILES)
+            both[n] = held("both%d" % n, [P, PACK * TILE], F32, place)
+            engine.tensor_tensor(both[n][:], part(gate[half], i), part(stance[half], i), MULT)
+
+        third, h_codes, h_plane = {}, {}, {}
+        width = 2 * TILE
+
+        def multiply(n):
+            third[n] = product(3, 1, *divmod(n, TILES))
+
+        def combine(n):
+            nc.vector.tensor_tensor(woven(part(h[n // 2], n % 2)), third[n], woven(both[n][:]), MULT)
+
+        def quantize_h(q):
+            h_codes[q] = held("h_codes%d" % q, [P, width], I32)
+            h_plane[q] = held("h_plane%d" % q, [P, width], U8)
+            nc.vector.quantize_mx(out=h_codes[q][:].bitcast(FP8X4), scales=h_plane[q][:], in_=h[q][:])
+
+        def score(q, c, sums):
+            nc.tensor.matmul_mx(
+                out=sums,
+                lhsT=w4_codes[:, 2 * P * c : 2 * P * (c + 1)].bitcast(FP4X4),
+                lhsT_scale=w4_plane[:, P * c : P * (c + 1)],
+                rhs=h_codes[q][:].bitcast(FP8X4),
+                rhs_scale=h_plane[q][:],
+                start=True,
+                stop=True,
+            )
 
         def finish(q):
-            width = 2 * TILE
-            h_codes = held("h_codes%d" % q, [P, width], I32)
-            h_plane = held("h_plane%d" % q, [P, width], U8)
-            nc.vector.quantize_mx(out=h_codes[:].bitcast(FP8X4), scales=h_plane[:], in_=h[q][:])
             last = psum.tile([P, N // P, width], F32, name="last", tag="last", bufs=1)
-            for c in range(N // P):
-                nc.tensor.matmul_mx(
-                    out=last[:, c, :],
-                    lhsT=w4_codes[:, 2 * P * c : 2 * P * (c + 1)].bitcast(FP4X4),
-                    lhsT_scale=w4_plane[:, P * c : P * (c + 1)],
-                    rhs=h_codes[:].bitcast(FP8X4),
-                    rhs_scale=h_plane[:],
-                    start=True,
-                    stop=True,
-                )
             result = held("result%d" % q, [P, N // P, width], F32)
+            for c in range(N // P):
+                score(q, c, last[:, c, :])
             for c in range(N // P):
                 nc.scalar.activation(out=result[:, c, :], in_=last[:, c, :], func=ACT.Identity, bias=bias[:, c : c + 1])
             nc.sync.dma_start(
                 out=out.rearrange("(c p) j -> p c j", p=P)[:, :, q * width : (q + 1) * width], in_=result[:]
             )
 
-        nc.sync.dma_start(citing[:], offs)
+        def finish_last(q):
+            for c in range(N // P):
+                last = psum.tile([P, width], F32, name="bank", tag="bank", bufs=7)
+                score(q, c, last[:])
+                result = held("result%d%d" % (q, c), [P, width], F32)
+                if c == 0:
+                    nc.vector.tensor_scalar(result[:], last[:], bias[:, c : c + 1], None, ADD)
+                else:
+                    nc.scalar.activation(out=result[:], in_=last[:], func=ACT.Identity, bias=bias[:, c : c + 1])
+                nc.sync.dma_start(out=out[c * P : (c + 1) * P, q * width : (q + 1) * width], in_=result[:])
+
         load_table(0)
+        nc.sync.dma_start(citing[:], offs)
         nc.sync.dma_start(retracted[:], offs2)
         rows = tab_scales.bitcast(I32).rearrange("a (q r) c -> r q a c", r=4)
         for r in range(4):
@@ -208,7 +227,7 @@ def tile_list_retraction_exposure_scores_kernel(
         w4_codes = held("w4_codes", [P, 2 * N], U8, rounded_place[1, 1] + 1024)
         w4_plane = held("w4_plane", [P, N], U8, rounded_place[1, 1] + 1536)
         bias = held("bias", [P, N // P], F32, rounded_place[1, 1] + 1792)
-        nc.vector.memset(w4_plane[:].bitcast(I32), 0)
+        nc.gpsimd.memset(w4_plane[:].bitcast(I32), 0)
         nc.sync.dma_start(out=w4_codes[:].bitcast(I32), in_=w4_words[0].bitcast(I32))
         for q in range(4):
             nc.sync.dma_start(
@@ -217,8 +236,14 @@ def tile_list_retraction_exposure_scores_kernel(
         with nc.allow_non_contiguous_dma(reason="one bias value a partition"):
             nc.sync.dma_start(out=bias[:], in_=bo.rearrange("(c p) -> p c", p=P))
 
-        reorder(w2_planes, w2_raw_scales)
-        reorder(w2_codes, w2_raw)
+        nc.vector.tensor_copy(
+            out=w2_planes[:].rearrange("p (a t m) -> p a t m", a=PASSES, t=PACK),
+            in_=w2_raw_scales[:].rearrange("p (a m t) -> p a t m", a=PASSES, t=PACK),
+        )
+        nc.vector.tensor_copy(
+            out=w2_codes[:].rearrange("p (a u v m) -> p a u m v", a=PASSES, u=2, v=2),
+            in_=w2_raw[:].rearrange("p (a m u v) -> p a u m v", a=PASSES, u=2, v=2),
+        )
         for a in range(PASSES):
             codes[2, a] = w2_codes[:, a * H : (a + 1) * H]
             scales[2, a] = w2_planes[:, a * H : (a + 1) * H]
@@ -238,17 +263,37 @@ def tile_list_retraction_exposure_scores_kernel(
             activate(stance[1], 1, 0, ACT.Tanh, 1, i)
         activate(gate[1], 2, 1, ACT.Silu, 1, 0)
         activate(gate[1], 2, 1, ACT.Silu, 1, 1)
-        combine(0, 0, nc.vector, rounded_place[3, 1] + 0)
+        multiply(0)
         activate(gate[1], 2, 1, ACT.Silu, 1, 2)
-        combine(0, 1, nc.vector, rounded_place[3, 1] + 2048)
+        multiply(1)
         activate(gate[1], 2, 1, ACT.Silu, 1, 3)
-        combine(0, 2, nc.vector, rounded_place[3, 0] + 0)
+        multiply(2)
+        multiply(3)
+        pair(0, nc.vector, rounded_place[3, 1] + 0)
+        pair(1, nc.vector, rounded_place[3, 1] + 2048)
+        combine(0)
+        pair(2, nc.vector, rounded_place[3, 0] + 0)
+        combine(1)
+        pair(3, nc.vector, rounded_place[3, 0] + 2048)
+        quantize_h(0)
+        multiply(4)
+        multiply(5)
         finish(0)
-        combine(0, 3, nc.vector, rounded_place[3, 0] + 2048)
-        combine(1, 0, nc.vector)
+        combine(2)
+        pair(4, nc.vector)
+        combine(3)
+        pair(5, nc.vector)
+        quantize_h(1)
+        multiply(6)
+        multiply(7)
         finish(1)
-        combine(1, 1, nc.vector)
-        combine(1, 2, nc.vector)
+        combine(4)
+        pair(6, nc.vector)
+        combine(5)
+        pair(7, nc.vector)
+        quantize_h(2)
         finish(2)
-        combine(1, 3, nc.vector)
-        finish(3)
+        combine(6)
+        combine(7)
+        quantize_h(3)
+        finish_last(3)

@@ -19,20 +19,33 @@ ADD = mybir.AluOpType.add
 P = 128
 PACK = 4
 PASSES = K // (P * PACK)
-HALF = 512
+HALF = S // 2
 TILE = 128
 TILES = HALF // TILE
-LIVE = 100
+QUARTER = 2 * TILE
+QUARTERS = S // QUARTER
+CITING, RETRACTED = 0, 1
+QUADRANT = 32
+ROWS = 4
 SHIFT = 16
+LIVE = 3 * QUADRANT + ROWS
+BANKS = 7
 
-TABLE_B = 0
-W2_SCALES = 8192
-RAW_B = 9216
-RAW_A = RAW_B + 8192
-RAW_LAST = RAW_A + 8192
-SCALE_TABLE = RAW_LAST + 8192 - 64
-W2_RAW = SCALE_TABLE + 3712
-ROUNDED = W2_RAW + 4096
+EDGE = 64
+RAW_BYTES = 4 * PACK * H
+ROUNDED_BYTES = 2 * PACK * H
+CODE_BYTES = 4 * H
+WORD_BYTES = 2 * HALF
+TABLE_1 = 0
+W2_SCALES = TABLE_1 + RAW_BYTES
+RAW_B = W2_SCALES + PASSES * H
+RAW_A = RAW_B + RAW_BYTES
+RAW_LAST = RAW_A + RAW_BYTES
+SCALE_TABLE = RAW_LAST + RAW_BYTES - EDGE
+FIRST_CODES = SCALE_TABLE + 2 * EDGE
+FIRST_WORDS = FIRST_CODES + CODE_BYTES + H
+W2_WORDS = FIRST_WORDS + WORD_BYTES
+ROUNDED = W2_WORDS + PASSES * CODE_BYTES
 
 
 def tile_list_retraction_exposure_scores_kernel(
@@ -52,11 +65,13 @@ def tile_list_retraction_exposure_scores_kernel(
         citing = keep.tile([P, S // 16], U16, name="citing")
         retracted = keep.tile([P, S // 16], U16, name="retracted")
         lists = (citing, retracted)
-        idle_in = held("idle_in", [P, 32], F32, RAW_A - 64)
-        idle_out = held("idle_out", [P, 32], F32, W2_SCALES - 64)
-        nc.gpsimd.memset(idle_in[:], 0.0)
-        nc.scalar.activation(out=idle_out[:], in_=idle_in[:], func=ACT.Silu)
-        table = [held("table0", [P, T], U16), held("table1", [P, T], U16, TABLE_B)]
+
+        warm_in = held("idle_in", [P, 2 * EDGE // 4], F32, RAW_A - EDGE)
+        warm_out = held("idle_out", [P, 2 * EDGE // 4], F32, W2_SCALES - EDGE)
+        nc.gpsimd.memset(warm_in[:], 0.0)
+        nc.scalar.activation(out=warm_out[:], in_=warm_in[:], func=ACT.Silu)
+
+        table = [held("table0", [P, T], U16), held("table1", [P, T], U16, TABLE_1)]
         table_scales = held("table_scales", [P, T], U8, SCALE_TABLE)
         picked_scales = held("picked_scales", [P, 2 * S], U8)
         moved_scales = held("moved_scales", [P, 2 * S], U8)
@@ -65,7 +80,7 @@ def tile_list_retraction_exposure_scores_kernel(
         w2_planes = held("w2_planes", [P, PASSES * H], U8)
         planes = (picked_scales, moved_scales)
         raw, words, rounded, codes, scales, gate, stance = {}, {}, {}, {}, {}, {}, {}
-        rounded_place = {(w, a): ROUNDED + 4096 * (w - 1 + a) for w in (1, 3) for a in range(PASSES)}
+        rounded_place = {key: ROUNDED + ROUNDED_BYTES * n for n, key in enumerate(((1, 0), (1, 1), (3, 0), (3, 1)))}
 
         nc.vector.memset(table_scales[:].bitcast(I32), 0)
         nc.vector.memset(moved_scales[:].bitcast(I32), 0)
@@ -93,31 +108,31 @@ def tile_list_retraction_exposure_scores_kernel(
             )
 
         def quantize(w, a, place=None):
-            c = held("codes%d%d" % (w, a), [P, H], I32, place)
-            s = held("scales%d%d" % (w, a), [P, H], U8, None if place is None else place + 2048)
-            nc.vector.quantize_mx(out=c[:].bitcast(FP8X4), scales=s[:], in_=rounded[w, a][:])
-            codes[w, a], scales[w, a] = c[:], s[:]
+            packed = held("codes%d%d" % (w, a), [P, H], I32, place)
+            plane = held("scales%d%d" % (w, a), [P, H], U8, None if place is None else place + CODE_BYTES)
+            nc.vector.quantize_mx(out=packed[:].bitcast(FP8X4), scales=plane[:], in_=rounded[w, a][:])
+            codes[w, a], scales[w, a] = packed[:], plane[:]
 
-        def product(w, which, half, i):
-            bank = psum.tile([P, PACK, TILE], F32, name="bank", tag="bank", bufs=7)
-            cols = slice(i * TILE, (i + 1) * TILE)
-            start = which * S + half * HALF + i * TILE
-            for t in range(PACK):
-                m = slice(t * P, (t + 1) * P)
-                for a in range(PASSES):
-                    nc.tensor.matmul_mx(
-                        out=bank[:, t, :],
-                        lhsT=codes[w, a][:, m].bitcast(FP8X4),
-                        lhsT_scale=scales[w, a][:, m],
-                        rhs=words[which, a, half][:, cols].bitcast(FP4X4),
-                        rhs_scale=planes[a][:, start : start + TILE],
-                        start=(a == 0),
-                        stop=(a == PASSES - 1),
-                    )
-            return bank[:].rearrange("p t n -> p n t")
+        def products(w, which, half, tiles):
+            banks = [psum.tile([P, PACK, TILE], F32, name="bank", tag="bank", bufs=BANKS) for i in tiles]
+            for a in range(PASSES):
+                for i, bank in zip(tiles, banks):
+                    start = which * S + half * HALF + i * TILE
+                    for t in range(PACK):
+                        m = slice(t * P, (t + 1) * P)
+                        nc.tensor.matmul_mx(
+                            out=bank[:, t, :],
+                            lhsT=codes[w, a][:, m].bitcast(FP8X4),
+                            lhsT_scale=scales[w, a][:, m],
+                            rhs=words[which, a, half][:, i * TILE : (i + 1) * TILE].bitcast(FP4X4),
+                            rhs_scale=planes[a][:, start : start + TILE],
+                            start=(a == 0 and t == 0),
+                            stop=(a == PASSES - 1 and t == PACK - 1),
+                        )
+            return [bank[:].rearrange("p t n -> p n t") for bank in banks]
 
-        def woven(tile):
-            return tile.rearrange("p (n t) -> p n t", t=PACK)
+        def woven(columns):
+            return columns.rearrange("p (n t) -> p n t", t=PACK)
 
         def values(name, place=None):
             return held(name, [P, PACK * HALF], F32, place)
@@ -125,30 +140,29 @@ def tile_list_retraction_exposure_scores_kernel(
         def part(tile, i):
             return tile[:, i * PACK * TILE : (i + 1) * PACK * TILE]
 
-        def activate(into, w, which, func, half, i):
-            nc.scalar.activation(out=woven(part(into, i)), in_=product(w, which, half, i), func=func)
+        def activate(into, w, which, func, half, tiles):
+            for i, sums in zip(tiles, products(w, which, half, tiles)):
+                nc.scalar.activation(out=woven(part(into, i)), in_=sums, func=func)
 
-        h = [held("h%d" % q, [P, PACK * 2 * TILE], BF16) for q in range(4)]
+        h = [held("h%d" % q, [P, PACK * QUARTER], BF16) for q in range(QUARTERS)]
+        both, third, h_codes, h_plane = {}, {}, {}, {}
 
-        both = {}
-
-        def pair(n, engine, place=None):
+        def pair(n):
             half, i = divmod(n, TILES)
+            place = rounded_place[3, 1 - n // 2] + CODE_BYTES * (n % 2) if half == 0 else None
             both[n] = held("both%d" % n, [P, PACK * TILE], F32, place)
-            engine.tensor_tensor(both[n][:], part(gate[half], i), part(stance[half], i), MULT)
-
-        third, h_codes, h_plane = {}, {}, {}
-        width = 2 * TILE
+            nc.vector.tensor_tensor(both[n][:], part(gate[half], i), part(stance[half], i), MULT)
 
         def multiply(n):
-            third[n] = product(3, 1, *divmod(n, TILES))
+            half, i = divmod(n, TILES)
+            third[n] = products(3, RETRACTED, half, [i])[0]
 
         def combine(n):
             nc.vector.tensor_tensor(woven(part(h[n // 2], n % 2)), third[n], woven(both[n][:]), MULT)
 
         def quantize_h(q):
-            h_codes[q] = held("h_codes%d" % q, [P, width], I32)
-            h_plane[q] = held("h_plane%d" % q, [P, width], U8)
+            h_codes[q] = held("h_codes%d" % q, [P, QUARTER], I32)
+            h_plane[q] = held("h_plane%d" % q, [P, QUARTER], U8)
             nc.vector.quantize_mx(out=h_codes[q][:].bitcast(FP8X4), scales=h_plane[q][:], in_=h[q][:])
 
         def score(q, c, sums):
@@ -163,75 +177,78 @@ def tile_list_retraction_exposure_scores_kernel(
             )
 
         def finish(q):
-            last = psum.tile([P, N // P, width], F32, name="last", tag="last", bufs=1)
-            result = held("result%d" % q, [P, N // P, width], F32)
+            last = psum.tile([P, N // P, QUARTER], F32, name="last", tag="last", bufs=1)
+            result = held("result%d" % q, [P, N // P, QUARTER], F32)
             for c in range(N // P):
                 score(q, c, last[:, c, :])
             for c in range(N // P):
                 nc.scalar.activation(out=result[:, c, :], in_=last[:, c, :], func=ACT.Identity, bias=bias[:, c : c + 1])
             nc.sync.dma_start(
-                out=out.rearrange("(c p) j -> p c j", p=P)[:, :, q * width : (q + 1) * width], in_=result[:]
+                out=out.rearrange("(c p) j -> p c j", p=P)[:, :, q * QUARTER : (q + 1) * QUARTER], in_=result[:]
             )
 
         def finish_last(q):
             for c in range(N // P):
-                last = psum.tile([P, width], F32, name="bank", tag="bank", bufs=7)
+                last = psum.tile([P, QUARTER], F32, name="bank", tag="bank", bufs=BANKS)
                 score(q, c, last[:])
-                result = held("result%d%d" % (q, c), [P, width], F32)
+                result = held("result%d%d" % (q, c), [P, QUARTER], F32)
                 if c == 0:
                     nc.vector.tensor_scalar(result[:], last[:], bias[:, c : c + 1], None, ADD)
                 else:
                     nc.scalar.activation(out=result[:], in_=last[:], func=ACT.Identity, bias=bias[:, c : c + 1])
-                nc.sync.dma_start(out=out[c * P : (c + 1) * P, q * width : (q + 1) * width], in_=result[:])
+                nc.sync.dma_start(out=out[c * P : (c + 1) * P, q * QUARTER : (q + 1) * QUARTER], in_=result[:])
 
         load_table(0)
         nc.sync.dma_start(citing[:], offs)
         nc.sync.dma_start(retracted[:], offs2)
-        rows = tab_scales.bitcast(I32).rearrange("a (q r) c -> r q a c", r=4)
-        for r in range(4):
-            nc.sync.dma_start(out=table_scales[r:P:SHIFT, :].bitcast(I32), in_=rows[r])
+        table_rows = tab_scales.bitcast(I32).rearrange("a (q r) c -> r q a c", r=ROWS)
+        for r in range(ROWS):
+            nc.sync.dma_start(out=table_scales[r:P:SHIFT, :].bitcast(I32), in_=table_rows[r])
         load_weight(1, 0, RAW_A)
         load_weight(1, 1, RAW_B)
         load_table(1)
-        rows = w2_scales.bitcast(I32).rearrange("a r c -> r a c")
-        for q in range(4):
+        w2_rows = w2_scales.bitcast(I32).rearrange("a r c -> r a c")
+        for q in range(P // QUADRANT):
             nc.sync.dma_start(
-                out=w2_raw_scales[32 * q : 32 * q + 4, :].bitcast(I32).rearrange("p (a c) -> p a c", a=PASSES),
-                in_=rows[4 * q : 4 * q + 4],
+                out=w2_raw_scales[QUADRANT * q : QUADRANT * q + ROWS, :]
+                .bitcast(I32)
+                .rearrange("p (a c) -> p a c", a=PASSES),
+                in_=w2_rows[ROWS * q : ROWS * (q + 1)],
             )
 
-        gather_words(0, 0, 0)
-        gather_words(1, 0, 0)
+        gather_words(CITING, 0, 0)
+        gather_words(RETRACTED, 0, 0)
         cast(1, 0)
         load_weight(3, 0, RAW_A)
         cast(1, 1)
-        for which in range(2):
+        for which in (CITING, RETRACTED):
             nc.vector.tensor_copy(picked_scales[:, which * S : (which + 1) * S], table_scales[:].indirect(lists[which][:]))
         nc.sync.dma_start(
             out=moved_scales[0:LIVE, :].bitcast(I32), in_=picked_scales[SHIFT : SHIFT + LIVE, :].bitcast(I32)
         )
-        w2_raw = held("w2_raw", [P, PASSES * H], I32, W2_RAW)
+        w2_raw = held("w2_raw", [P, PASSES * H], I32, W2_WORDS)
         nc.sync.dma_start(
             out=w2_raw[:].rearrange("p (a c) -> p a c", a=PASSES),
             in_=w2_words.rearrange("a p c i -> p a (c i)").bitcast(I32),
         )
         load_weight(3, 1, RAW_LAST)
-        quantize(1, 0, SCALE_TABLE + 128)
-        gather_words(0, 1, 0, SCALE_TABLE + 2688)
+        quantize(1, 0, FIRST_CODES)
+        gather_words(CITING, 1, 0, FIRST_WORDS)
         quantize(1, 1)
         stance[0] = values("stance0")
-        for i in range(TILES):
-            activate(stance[0], 1, 0, ACT.Tanh, 0, i)
-        gather_words(1, 1, 0, rounded_place[1, 1])
+        activate(stance[0], 1, CITING, ACT.Tanh, 0, range(TILES))
 
-        w4_codes = held("w4_codes", [P, 2 * N], U8, rounded_place[1, 1] + 1024)
-        w4_plane = held("w4_plane", [P, N], U8, rounded_place[1, 1] + 1536)
-        bias = held("bias", [P, N // P], F32, rounded_place[1, 1] + 1792)
+        freed = rounded_place[1, 1]
+        gather_words(RETRACTED, 1, 0, freed)
+        w4_codes = held("w4_codes", [P, 2 * N], U8, freed + WORD_BYTES)
+        w4_plane = held("w4_plane", [P, N], U8, freed + WORD_BYTES + 2 * N)
+        bias = held("bias", [P, N // P], F32, freed + WORD_BYTES + 3 * N)
         nc.gpsimd.memset(w4_plane[:].bitcast(I32), 0)
         nc.sync.dma_start(out=w4_codes[:].bitcast(I32), in_=w4_words[0].bitcast(I32))
-        for q in range(4):
+        for q in range(P // QUADRANT):
             nc.sync.dma_start(
-                out=w4_plane[32 * q : 32 * q + 4, :].bitcast(I32), in_=w4_scales[0].bitcast(I32)[4 * q : 4 * q + 4, :]
+                out=w4_plane[QUADRANT * q : QUADRANT * q + ROWS, :].bitcast(I32),
+                in_=w4_scales[0].bitcast(I32)[ROWS * q : ROWS * (q + 1), :],
             )
         with nc.allow_non_contiguous_dma(reason="one bias value a partition"):
             nc.sync.dma_start(out=bias[:], in_=bo.rearrange("(c p) -> p c", p=P))
@@ -247,53 +264,39 @@ def tile_list_retraction_exposure_scores_kernel(
         for a in range(PASSES):
             codes[2, a] = w2_codes[:, a * H : (a + 1) * H]
             scales[2, a] = w2_planes[:, a * H : (a + 1) * H]
+
         cast(3, 0)
         cast(3, 1)
-        gate[0] = values("gate0", RAW_LAST + 64)
+        gate[0] = values("gate0", RAW_LAST + EDGE)
         for i in range(TILES):
-            activate(gate[0], 2, 1, ACT.Silu, 0, i)
-        for which in range(2):
+            activate(gate[0], 2, RETRACTED, ACT.Silu, 0, [i])
+        for which in (CITING, RETRACTED):
             for a in range(PASSES):
-                gather_words(which, a, 1, W2_RAW + 1024 * (2 * which + a))
+                gather_words(which, a, 1, W2_WORDS + WORD_BYTES * (PASSES * which + a))
         quantize(3, 0)
         quantize(3, 1)
-        stance[1] = values("stance1", RAW_A + 64)
+        stance[1] = values("stance1", RAW_A + EDGE)
         gate[1] = values("gate1")
         for i in range(TILES):
-            activate(stance[1], 1, 0, ACT.Tanh, 1, i)
-        activate(gate[1], 2, 1, ACT.Silu, 1, 0)
-        activate(gate[1], 2, 1, ACT.Silu, 1, 1)
-        multiply(0)
-        activate(gate[1], 2, 1, ACT.Silu, 1, 2)
-        multiply(1)
-        activate(gate[1], 2, 1, ACT.Silu, 1, 3)
-        multiply(2)
-        multiply(3)
-        pair(0, nc.vector, rounded_place[3, 1] + 0)
-        pair(1, nc.vector, rounded_place[3, 1] + 2048)
-        combine(0)
-        pair(2, nc.vector, rounded_place[3, 0] + 0)
-        combine(1)
-        pair(3, nc.vector, rounded_place[3, 0] + 2048)
-        quantize_h(0)
-        multiply(4)
-        multiply(5)
-        finish(0)
-        combine(2)
-        pair(4, nc.vector)
-        combine(3)
-        pair(5, nc.vector)
-        quantize_h(1)
-        multiply(6)
-        multiply(7)
-        finish(1)
-        combine(4)
-        pair(6, nc.vector)
-        combine(5)
-        pair(7, nc.vector)
-        quantize_h(2)
-        finish(2)
-        combine(6)
-        combine(7)
-        quantize_h(3)
-        finish_last(3)
+            activate(stance[1], 1, CITING, ACT.Tanh, 1, [i])
+
+        activate(gate[1], 2, RETRACTED, ACT.Silu, 1, [0])
+        for i in range(1, TILES):
+            activate(gate[1], 2, RETRACTED, ACT.Silu, 1, [i])
+            multiply(i - 1)
+        multiply(TILES - 1)
+
+        pair(0)
+        pair(1)
+        for q in range(QUARTERS - 1):
+            for n in (2 * q, 2 * q + 1):
+                combine(n)
+                pair(n + 2)
+            quantize_h(q)
+            for n in range(2 * q + TILES, min(2 * q + TILES + 2, 2 * TILES)):
+                multiply(n)
+            finish(q)
+        combine(2 * TILES - 2)
+        combine(2 * TILES - 1)
+        quantize_h(QUARTERS - 1)
+        finish_last(QUARTERS - 1)

from contextlib import ExitStack

import concourse.mybir as mybir

K, H, N, T, S = 1024, 512, 256, 4096, 1024
FLOPS = 2 * S * (3 * K * H + H * N)

F32 = mybir.dt.float32
BF16 = mybir.dt.bfloat16
I32 = mybir.dt.int32
U16 = mybir.dt.uint16
U8 = mybir.dt.uint8
FP8X4 = mybir.dt.float8_e4m3fn_x4
FP4X4 = mybir.dt.float4_e2m1fn_x4
ACT = mybir.ActivationFunctionType
MULT = mybir.AluOpType.mult
ADD = mybir.AluOpType.add

P = 128
PACK = 4
PASSES = K // (P * PACK)
HALF = S // 2
TILE = 128
TILES = HALF // TILE
QUARTER = 2 * TILE
QUARTERS = S // QUARTER
CITING, RETRACTED = 0, 1
QUADRANT = 32
ROWS = 4
SHIFT = 16
LIVE = 3 * QUADRANT + ROWS
BANKS = 7

EDGE = 64
RAW_BYTES = 4 * PACK * H
ROUNDED_BYTES = 2 * PACK * H
CODE_BYTES = 4 * H
WORD_BYTES = 2 * HALF
TABLE_1 = 0
W2_SCALES = TABLE_1 + RAW_BYTES
RAW_B = W2_SCALES + PASSES * H
RAW_A = RAW_B + RAW_BYTES
RAW_LAST = RAW_A + RAW_BYTES
SCALE_TABLE = RAW_LAST + RAW_BYTES - EDGE
FIRST_CODES = SCALE_TABLE + 2 * EDGE
FIRST_WORDS = FIRST_CODES + CODE_BYTES + H
W2_WORDS = FIRST_WORDS + WORD_BYTES
ROUNDED = W2_WORDS + PASSES * CODE_BYTES


def tile_list_retraction_exposure_scores_kernel(
    tc, tab_words, tab_scales, offs, offs2, w1, w2_words, w2_scales, w3, w4_words, w4_scales, bo, out
):
    nc = tc.nc
    with ExitStack() as ctx:
        keep = ctx.enter_context(tc.tile_pool(name="keep", bufs=1))
        reused = ctx.enter_context(tc.tile_pool(name="reused", bufs=1))
        psum = ctx.enter_context(tc.psum_pool(name="psum", bufs=1))

        def held(name, shape, dtype, place=None):
            if place is None:
                return keep.tile(shape, dtype, name=name, align_bytes=64)
            return reused.tile(shape, dtype, name=name, align_bytes=64, offset=place)

        citing = keep.tile([P, S // 16], U16, name="citing")
        retracted = keep.tile([P, S // 16], U16, name="retracted")
        lists = (citing, retracted)

        warm_in = held("idle_in", [P, 2 * EDGE // 4], F32, RAW_A - EDGE)
        warm_out = held("idle_out", [P, 2 * EDGE // 4], F32, W2_SCALES - EDGE)
        nc.gpsimd.memset(warm_in[:], 0.0)
        nc.scalar.activation(out=warm_out[:], in_=warm_in[:], func=ACT.Silu)

        table = [held("table0", [P, T], U16), held("table1", [P, T], U16, TABLE_1)]
        table_scales = held("table_scales", [P, T], U8, SCALE_TABLE)
        picked_scales = held("picked_scales", [P, 2 * S], U8)
        moved_scales = held("moved_scales", [P, 2 * S], U8)
        w2_raw_scales = held("w2_raw_scales", [P, PASSES * H], U8, W2_SCALES)
        w2_codes = held("w2_codes", [P, PASSES * H], I32)
        w2_planes = held("w2_planes", [P, PASSES * H], U8)
        planes = (picked_scales, moved_scales)
        raw, words, rounded, codes, scales, gate, stance = {}, {}, {}, {}, {}, {}, {}
        rounded_place = {key: ROUNDED + ROUNDED_BYTES * n for n, key in enumerate(((1, 0), (1, 1), (3, 0), (3, 1)))}

        nc.vector.memset(table_scales[:].bitcast(I32), 0)
        nc.vector.memset(moved_scales[:].bitcast(I32), 0)
        nc.vector.memset(w2_raw_scales[:].bitcast(I32), 0)

        def load_table(a):
            nc.sync.dma_start(out=table[a][:].bitcast(I32), in_=tab_words[a].bitcast(I32))

        def load_weight(w, a, place):
            raw[w, a] = held("raw%d%d" % (w, a), [P, PACK, H], F32, place)
            rows = (w1 if w == 1 else w3)[a * P * PACK : (a + 1) * P * PACK, :]
            nc.sync.dma_start(out=raw[w, a][:], in_=rows.rearrange("(p j) c -> p j c", j=PACK))

        def gather_words(which, a, half, place=None):
            picked = held("words%d%d%d" % (which, a, half), [P, HALF], U16, place)
            piece = lists[which][:, half * HALF // 16 : (half + 1) * HALF // 16]
            nc.vector.tensor_copy(picked[:], table[a][:].indirect(piece))
            words[which, a, half] = picked

        def cast(w, a):
            rounded[w, a] = held("rounded%d%d" % (w, a), [P, PACK * H], BF16, rounded_place[w, a])
            nc.scalar.copy(
                out=rounded[w, a][:].rearrange("p (u v m j) -> p u m j v", u=2, v=2, j=PACK),
                in_=raw[w, a][:].rearrange("p j (m u v) -> p u m j v", u=2, v=2),
            )

        def quantize(w, a, place=None):
            packed = held("codes%d%d" % (w, a), [P, H], I32, place)
            plane = held("scales%d%d" % (w, a), [P, H], U8, None if place is None else place + CODE_BYTES)
            nc.vector.quantize_mx(out=packed[:].bitcast(FP8X4), scales=plane[:], in_=rounded[w, a][:])
            codes[w, a], scales[w, a] = packed[:], plane[:]

        def products(w, which, half, tiles):
            banks = [psum.tile([P, PACK, TILE], F32, name="bank", tag="bank", bufs=BANKS) for i in tiles]
            for a in range(PASSES):
                for i, bank in zip(tiles, banks):
                    start = which * S + half * HALF + i * TILE
                    for t in range(PACK):
                        m = slice(t * P, (t + 1) * P)
                        nc.tensor.matmul_mx(
                            out=bank[:, t, :],
                            lhsT=codes[w, a][:, m].bitcast(FP8X4),
                            lhsT_scale=scales[w, a][:, m],
                            rhs=words[which, a, half][:, i * TILE : (i + 1) * TILE].bitcast(FP4X4),
                            rhs_scale=planes[a][:, start : start + TILE],
                            start=(a == 0 and t == 0),
                            stop=(a == PASSES - 1 and t == PACK - 1),
                        )
            return [bank[:].rearrange("p t n -> p n t") for bank in banks]

        def woven(columns):
            return columns.rearrange("p (n t) -> p n t", t=PACK)

        def values(name, place=None):
            return held(name, [P, PACK * HALF], F32, place)

        def part(tile, i):
            return tile[:, i * PACK * TILE : (i + 1) * PACK * TILE]

        def activate(into, w, which, func, half, tiles):
            for i, sums in zip(tiles, products(w, which, half, tiles)):
                nc.scalar.activation(out=woven(part(into, i)), in_=sums, func=func)

        h = [held("h%d" % q, [P, PACK * QUARTER], BF16) for q in range(QUARTERS)]
        both, third, h_codes, h_plane = {}, {}, {}, {}

        def pair(n):
            half, i = divmod(n, TILES)
            place = rounded_place[3, 1 - n // 2] + CODE_BYTES * (n % 2) if half == 0 else None
            both[n] = held("both%d" % n, [P, PACK * TILE], F32, place)
            nc.vector.tensor_tensor(both[n][:], part(gate[half], i), part(stance[half], i), MULT)

        def multiply(n):
            half, i = divmod(n, TILES)
            third[n] = products(3, RETRACTED, half, [i])[0]

        def combine(n):
            nc.vector.tensor_tensor(woven(part(h[n // 2], n % 2)), third[n], woven(both[n][:]), MULT)

        def quantize_h(q):
            h_codes[q] = held("h_codes%d" % q, [P, QUARTER], I32)
            h_plane[q] = held("h_plane%d" % q, [P, QUARTER], U8)
            nc.vector.quantize_mx(out=h_codes[q][:].bitcast(FP8X4), scales=h_plane[q][:], in_=h[q][:])

        def score(q, c, sums):
            nc.tensor.matmul_mx(
                out=sums,
                lhsT=w4_codes[:, 2 * P * c : 2 * P * (c + 1)].bitcast(FP4X4),
                lhsT_scale=w4_plane[:, P * c : P * (c + 1)],
                rhs=h_codes[q][:].bitcast(FP8X4),
                rhs_scale=h_plane[q][:],
                start=True,
                stop=True,
            )

        def finish(q):
            last = psum.tile([P, N // P, QUARTER], F32, name="last", tag="last", bufs=1)
            result = held("result%d" % q, [P, N // P, QUARTER], F32)
            for c in range(N // P):
                score(q, c, last[:, c, :])
            for c in range(N // P):
                nc.scalar.activation(out=result[:, c, :], in_=last[:, c, :], func=ACT.Identity, bias=bias[:, c : c + 1])
            nc.sync.dma_start(
                out=out.rearrange("(c p) j -> p c j", p=P)[:, :, q * QUARTER : (q + 1) * QUARTER], in_=result[:]
            )

        def finish_last(q):
            for c in range(N // P):
                last = psum.tile([P, QUARTER], F32, name="bank", tag="bank", bufs=BANKS)
                score(q, c, last[:])
                result = held("result%d%d" % (q, c), [P, QUARTER], F32)
                if c == 0:
                    nc.vector.tensor_scalar(result[:], last[:], bias[:, c : c + 1], None, ADD)
                else:
                    nc.scalar.activation(out=result[:], in_=last[:], func=ACT.Identity, bias=bias[:, c : c + 1])
                nc.sync.dma_start(out=out[c * P : (c + 1) * P, q * QUARTER : (q + 1) * QUARTER], in_=result[:])

        load_table(0)
        nc.sync.dma_start(citing[:], offs)
        nc.sync.dma_start(retracted[:], offs2)
        table_rows = tab_scales.bitcast(I32).rearrange("a (q r) c -> r q a c", r=ROWS)
        for r in range(ROWS):
            nc.sync.dma_start(out=table_scales[r:P:SHIFT, :].bitcast(I32), in_=table_rows[r])
        load_weight(1, 0, RAW_A)
        load_weight(1, 1, RAW_B)
        load_table(1)
        w2_rows = w2_scales.bitcast(I32).rearrange("a r c -> r a c")
        for q in range(P // QUADRANT):
            nc.sync.dma_start(
                out=w2_raw_scales[QUADRANT * q : QUADRANT * q + ROWS, :]
                .bitcast(I32)
                .rearrange("p (a c) -> p a c", a=PASSES),
                in_=w2_rows[ROWS * q : ROWS * (q + 1)],
            )

        gather_words(CITING, 0, 0)
        gather_words(RETRACTED, 0, 0)
        cast(1, 0)
        load_weight(3, 0, RAW_A)
        cast(1, 1)
        for which in (CITING, RETRACTED):
            nc.vector.tensor_copy(picked_scales[:, which * S : (which + 1) * S], table_scales[:].indirect(lists[which][:]))
        nc.sync.dma_start(
            out=moved_scales[0:LIVE, :].bitcast(I32), in_=picked_scales[SHIFT : SHIFT + LIVE, :].bitcast(I32)
        )
        w2_raw = held("w2_raw", [P, PASSES * H], I32, W2_WORDS)
        nc.sync.dma_start(
            out=w2_raw[:].rearrange("p (a c) -> p a c", a=PASSES),
            in_=w2_words.rearrange("a p c i -> p a (c i)").bitcast(I32),
        )
        load_weight(3, 1, RAW_LAST)
        quantize(1, 0, FIRST_CODES)
        gather_words(CITING, 1, 0, FIRST_WORDS)
        quantize(1, 1)
        stance[0] = values("stance0")
        activate(stance[0], 1, CITING, ACT.Tanh, 0, range(TILES))

        freed = rounded_place[1, 1]
        gather_words(RETRACTED, 1, 0, freed)
        w4_codes = held("w4_codes", [P, 2 * N], U8, freed + WORD_BYTES)
        w4_plane = held("w4_plane", [P, N], U8, freed + WORD_BYTES + 2 * N)
        bias = held("bias", [P, N // P], F32, freed + WORD_BYTES + 3 * N)
        nc.gpsimd.memset(w4_plane[:].bitcast(I32), 0)
        nc.sync.dma_start(out=w4_codes[:].bitcast(I32), in_=w4_words[0].bitcast(I32))
        for q in range(P // QUADRANT):
            nc.sync.dma_start(
                out=w4_plane[QUADRANT * q : QUADRANT * q + ROWS, :].bitcast(I32),
                in_=w4_scales[0].bitcast(I32)[ROWS * q : ROWS * (q + 1), :],
            )
        with nc.allow_non_contiguous_dma(reason="one bias value a partition"):
            nc.sync.dma_start(out=bias[:], in_=bo.rearrange("(c p) -> p c", p=P))

        nc.vector.tensor_copy(
            out=w2_planes[:].rearrange("p (a t m) -> p a t m", a=PASSES, t=PACK),
            in_=w2_raw_scales[:].rearrange("p (a m t) -> p a t m", a=PASSES, t=PACK),
        )
        nc.vector.tensor_copy(
            out=w2_codes[:].rearrange("p (a u v m) -> p a u m v", a=PASSES, u=2, v=2),
            in_=w2_raw[:].rearrange("p (a m u v) -> p a u m v", a=PASSES, u=2, v=2),
        )
        for a in range(PASSES):
            codes[2, a] = w2_codes[:, a * H : (a + 1) * H]
            scales[2, a] = w2_planes[:, a * H : (a + 1) * H]

        cast(3, 0)
        cast(3, 1)
        gate[0] = values("gate0", RAW_LAST + EDGE)
        for i in range(TILES):
            activate(gate[0], 2, RETRACTED, ACT.Silu, 0, [i])
        for which in (CITING, RETRACTED):
            for a in range(PASSES):
                gather_words(which, a, 1, W2_WORDS + WORD_BYTES * (PASSES * which + a))
        quantize(3, 0)
        quantize(3, 1)
        stance[1] = values("stance1", RAW_A + EDGE)
        gate[1] = values("gate1")
        for i in range(TILES):
            activate(stance[1], 1, CITING, ACT.Tanh, 1, [i])

        activate(gate[1], 2, RETRACTED, ACT.Silu, 1, [0])
        for i in range(1, TILES):
            activate(gate[1], 2, RETRACTED, ACT.Silu, 1, [i])
            multiply(i - 1)
        multiply(TILES - 1)

        pair(0)
        pair(1)
        for q in range(QUARTERS - 1):
            for n in (2 * q, 2 * q + 1):
                combine(n)
                pair(n + 2)
            quantize_h(q)
            for n in range(2 * q + TILES, min(2 * q + TILES + 2, 2 * TILES)):
                multiply(n)
            finish(q)
        combine(2 * TILES - 2)
        combine(2 * TILES - 1)
        quantize_h(QUARTERS - 1)
        finish_last(QUARTERS - 1)
